import numpy as np
import ml_dtypes


def mxq(x, axis, fmt="e4m3"):
    dtype, down = {"e4m3": (ml_dtypes.float8_e4m3fn, 7), "e5m2": (ml_dtypes.float8_e5m2, 14)}[fmt]
    v = np.moveaxis(np.asarray(x, np.float32).astype(ml_dtypes.bfloat16).astype(np.float64), axis, -1)
    blocks = v.reshape(v.shape[:-1] + (-1, 32))
    amax = np.abs(blocks).max(-1, keepdims=True)
    byte = np.maximum(np.where(amax > 0, np.frexp(amax)[1] - 1 + 127, 0) - down, 1)
    scale = np.exp2(byte - 127.0)
    codes = (blocks / scale).astype(np.float32).astype(dtype).astype(np.float64)
    return np.moveaxis((codes * scale).reshape(v.shape), -1, axis)


WIDE = False


def mx_kscale(k):
    if not WIDE:
        return np.ones(k)
    levels = np.array([10, -10, 5, -5, 0])
    if k % 512:
        return np.exp2(np.random.permutation(np.resize(levels, k // 32))).repeat(32)
    a = np.empty((k // 512, 16))
    for p in range(k // 512):
        a[p, :8] = np.random.permutation(np.resize(levels, 8))
        for g in range(8):
            far = levels[np.abs(levels - a[p, g]) >= 10]
            a[p, g + 8] = far[np.random.randint(len(far))]
    return np.exp2(a.ravel()).repeat(32)


def f64(x):
    return np.asarray(x).astype(np.float64)


def striped(idx):
    return np.tile(idx.reshape(-1, 16).T, (8, 1)).astype(np.uint16)


def unstriped(offs):
    return offs[:16].T.reshape(-1).astype(np.int64)


E2M1 = np.array([0.0, 0.5, 1.0, 1.5, 2.0, 3.0, 4.0, 6.0, -0.0, -0.5, -1.0, -1.5, -2.0, -3.0, -4.0, -6.0])


def pack_weight(w, fmt):
    k, n = w.shape
    w = f64(np.asarray(w, np.float32).astype(ml_dtypes.bfloat16)).reshape(k // 32, 32, n)
    amax = np.abs(w).max(1)
    if fmt == "e4m3":
        byte = np.frexp(amax)[1] - 1 + 127 - 7
    else:
        mant, ex = np.frexp(amax / 6.0)
        byte = np.where(mant > 0.5, ex, ex - 1) + 127
    byte = np.clip(np.where(amax > 0, byte, 1), 1, 254)
    scaled = (w * np.exp2(127.0 - byte)[:, None, :]).reshape(k, n).astype(np.float32)
    by_word = np.ascontiguousarray(scaled.reshape(k // 512, 128, 4, n).transpose(0, 1, 3, 2))
    if fmt == "e4m3":
        words = by_word.astype(ml_dtypes.float8_e4m3fn).view(np.uint8)
    else:
        c = by_word.astype(ml_dtypes.float4_e2m1fn).view(np.uint8) & 0xF
        words = (c[..., 0::2] | (c[..., 1::2] << 4)).reshape(k // 512, 128, 2 * n)
    return np.ascontiguousarray(words), np.ascontiguousarray(byte.astype(np.uint8).reshape(k // 512, 16, n))


def unpack_weight(words, scales, fmt):
    g, _, n = scales.shape
    words = np.ascontiguousarray(words).reshape(g, 128, n, -1)
    if fmt == "e4m3":
        vals = words.view(ml_dtypes.float8_e4m3fn).astype(np.float64)
    else:
        nib = np.empty((g, 128, n, 4), np.uint8)
        nib[..., 0::2] = words & 0xF
        nib[..., 1::2] = words >> 4
        vals = E2M1[nib]
    vals = vals * np.repeat(np.exp2(scales.astype(np.float64) - 127.0), 8, axis=1)[..., None]
    return vals.transpose(0, 1, 3, 2).reshape(g * 512, n)


def gelu(v):
    return 0.5 * v * (1.0 + np.tanh(np.sqrt(2.0 / np.pi) * (v + 0.044715 * v**3)))


K, T, S, H, N, T2 = 1024, 2048, 512, 512, 768, 1024

def setup_inputs():
    n = np.random.standard_normal
    s = mx_kscale(K)[:, None]
    u = mx_kscale(H)[:, None]
    tab_words, tab_scales = pack_weight(n((K, T)) * s, "e4m3")
    cand_w_words, cand_w_scales = pack_weight(1.5 * n((K, H)) / np.sqrt(K) / s, "e2m1")
    slot_w_words, slot_w_scales = pack_weight(2.5 * n((H, N)) / np.sqrt(H) / u, "e4m3")
    fam_w = 0.6 * n((K, H)) / np.sqrt(K) / s
    floor_w = 0.5 * n((K, H)) / np.sqrt(K) / s * u.T
    gain = 2.5 * np.exp(0.2 * n(H)) * u[:, 0]
    return {"tab_words": tab_words, "tab_scales": tab_scales,
            "offs": striped(np.random.permutation(T)[:S]),
            "offs2": striped(np.random.permutation(T)[:S]),
            "offs3": striped(np.random.permutation(T2)[:S]),
            "fam_w": fam_w.astype(np.float32),
            "cand_w_words": cand_w_words, "cand_w_scales": cand_w_scales,
            "floor_w": floor_w.astype(np.float32),
            "gain": gain.astype(np.float32),
            "slot_w_words": slot_w_words, "slot_w_scales": slot_w_scales,
            "d": (0.8 * n(N)).astype(np.float32),
            "wgo": np.exp(0.3 * n((128, S))).astype(np.float32)}

def reference(tab_words, tab_scales, offs, offs2, offs3, fam_w, cand_w_words, cand_w_scales,
              floor_w, gain, slot_w_words, slot_w_scales, d, wgo):
    TW = unpack_weight(tab_words, tab_scales, "e4m3")
    v = TW[:, unstriped(offs)]
    v2 = TW[:, unstriped(offs2)]
    fam = mxq(f64(fam_w), 0, "e4m3").T @ v
    cand = unpack_weight(cand_w_words, cand_w_scales, "e2m1").T @ v2
    low = mxq(f64(floor_w), 0, "e4m3").T @ v
    h = np.maximum(f64(gain)[:, None] * np.sin(fam) * np.tanh(cand), low)
    e = unpack_weight(slot_w_words, slot_w_scales, "e4m3").T @ mxq(h, 0, "e4m3")
    y = 1.0 / (1.0 + np.exp(-(e + f64(d)[:, None])))
    out = np.zeros((N, T2))
    out[:, unstriped(offs3)] = np.tile(f64(wgo), (N // 128, 1)) * y
    return out

@@ -1,0 +1,252 @@
+import math
+from contextlib import ExitStack
+
+import concourse.mybir as mybir
+from concourse.masks import make_identity
+
+K, T, S, H, N, T2 = 1024, 2048, 512, 512, 768, 1024
+FLOPS = 2 * S * (3 * K * H + H * N)
+
+F32 = mybir.dt.float32
+BF16 = mybir.dt.bfloat16
+I32 = mybir.dt.int32
+U32 = mybir.dt.uint32
+U16 = mybir.dt.uint16
+U8 = mybir.dt.uint8
+FP8X4 = mybir.dt.float8_e4m3fn_x4
+FP4X4 = mybir.dt.float4_e2m1fn_x4
+ACT = mybir.ActivationFunctionType
+ALU = mybir.AluOpType
+
+P = 128
+PACK = 4
+PASSES = K // (P * PACK)
+QUADS = 4
+CHUNK = 128
+CHUNKS = S // CHUNK
+ROW_TILES = N // P
+PAGES = 4
+
+
+def tile_list_host_family_slots_kernel(
+    tc, tab_words, tab_scales, offs, offs2, offs3, fam_w, cand_w_words, cand_w_scales,
+    floor_w, gain, slot_w_words, slot_w_scales, d, wgo, out,
+):
+    nc = tc.nc
+    with ExitStack() as ctx:
+        keep = ctx.enter_context(tc.tile_pool(name="keep", bufs=1))
+        ring = ctx.enter_context(tc.tile_pool(name="ring", bufs=2))
+        psum = ctx.enter_context(tc.psum_pool(name="psum", bufs=2))
+
+        def held(name, shape, dtype, tag=""):
+            return keep.tile(shape, dtype, name=name, tag=tag or name, align_bytes=64)
+
+        def quad_rows(q, first, count):
+            return slice(32 * q + first, 32 * q + first + count)
+
+        tab_sc_both = held("tab_sc_both", [P, T], U8, "first_scales_then_fam1")
+        tab_sc_last = held("tab_sc_last", [P, T], U8, "scratch1")
+        cand_w_sc = held("cand_w_sc", [P, PASSES, H], U8, "weight_scales")
+        nc.vector.memset(tab_sc_both[:].bitcast(I32), 0)
+        nc.vector.memset(tab_sc_last[:].bitcast(I32), 0)
+        nc.vector.memset(cand_w_sc[:].bitcast(I32), 0)
+        pages = [held("page%d" % i, [P, T2], F32) for i in range(PAGES)]
+        for page in pages[:2]:
+            nc.gpsimd.memset(page[:].bitcast(I32), 0)
+
+        fam_list = keep.tile([P, S // 16], U16, name="fam_list")
+        cand_list = keep.tile([P, S // 16], U16, name="cand_list")
+        slot_list = keep.tile([P, S // 16], U16, name="slot_list")
+
+        def load_weight(name, w, a, tag):
+            raw = held("%s_raw%d" % (name, a), [P, PACK, H], F32, tag)
+            nc.sync.dma_start(raw[:], w[a * P * PACK : (a + 1) * P * PACK, :].rearrange("(p j) c -> p j c", j=PACK))
+            return raw
+
+        def load_table(a):
+            words = held("tab_w%d" % a, [P, T], U32, "table%d" % a)
+            nc.sync.dma_start(words[:].bitcast(I32), tab_words[a].rearrange("p t i -> p (t i)").bitcast(I32))
+            return words
+
+        nc.sync.dma_start(cand_list[:], offs2)
+        nc.sync.dma_start(fam_list[:], offs)
+        tab_w = [load_table(0)]
+        fam_raw = [load_weight("fam", fam_w, 0, "fam0_then_floor1")]
+        tab_w.append(load_table(1))
+        cand_w = held("cand_w", [P, PASSES, 2 * H], U8, "cand_w_then_wgo")
+        nc.sync.dma_start(cand_w[:].bitcast(I32), cand_w_words.bitcast(I32).rearrange("a p b -> p a b"))
+        nc.sync.dma_start(slot_list[:], offs3)
+        tab_sc_hbm = tab_scales.bitcast(I32)
+        for q in range(QUADS):
+            nc.scalar.dma_start(tab_sc_both[quad_rows(q, 0, 8), :].bitcast(I32), tab_sc_hbm[:, 4 * q : 4 * q + 4, :])
+        for q in range(QUADS):
+            nc.scalar.dma_start(tab_sc_last[quad_rows(q, 0, 4), :].bitcast(I32), tab_sc_hbm[1, 4 * q : 4 * q + 4, :])
+        cand_sc_hbm = cand_w_scales.bitcast(I32)
+        for q in range(QUADS):
+            nc.scalar.dma_start(
+                cand_w_sc[quad_rows(q, 0, 4), :, :].bitcast(I32),
+                cand_sc_hbm[:, 4 * q : 4 * q + 4, :].rearrange("a r c -> r a c"),
+            )
+        gain_sb = keep.tile([P, PACK], F32, name="gain_sb")
+        nc.gpsimd.dma_start(gain_sb[:], gain.rearrange("(p t) -> p t", t=PACK))
+        d_sb = keep.tile([P, ROW_TILES], F32, name="d_sb")
+        with nc.allow_non_contiguous_dma(reason="one bias value to a partition"):
+            nc.gpsimd.dma_start(d_sb[:], d.rearrange("(c p) -> p c", p=P))
+
+
+        fam_sc = held("fam_sc", [P, S], U8)
+        cand_sc = [held("cand_sc%d" % a, [P, S], U8) for a in range(PASSES)]
+        nc.vector.tensor_copy(fam_sc[:], tab_sc_both[:].indirect(fam_list[:]))
+        nc.vector.tensor_copy(cand_sc[0][:], tab_sc_both[:].indirect(cand_list[:]))
+        fam_raw.append(load_weight("fam", fam_w, 1, "first_scales_then_fam1"))
+        for page in pages[2:]:
+            nc.vector.memset(page[:].bitcast(I32), 0)
+
+        def round_weight(a, raw, copy):
+            rounded = held("rounded%d" % a, [P, PACK, P, PACK], BF16, "scratch%d" % a)
+            copy(rounded[:].rearrange("p t m j -> p m j t"), raw[:].rearrange("p j (m t) -> p m j t", t=PACK))
+            return rounded
+
+        def quantise_weight(name, rounded):
+            codes = held(name + "_codes", [P, H], U32)
+            scales = held(name + "_scales", [P, H], U8)
+            nc.vector.quantize_mx(codes[:].bitcast(FP8X4), scales[:], rounded[:].rearrange("p t m j -> p (t m j)"))
+            return codes, scales
+
+        fam_bf = [round_weight(0, fam_raw[0], nc.scalar.copy)]
+
+        fam_v = [held("fam_v%d" % a, [P, S], U32) for a in range(PASSES)]
+        cand_v = [held("cand_v%d" % a, [P, S], U32) for a in range(PASSES)]
+        nc.vector.tensor_copy(cand_v[0][:], tab_w[0][:].indirect(cand_list[:]))
+        nc.vector.tensor_copy(fam_v[0][:], tab_w[0][:].indirect(fam_list[:]))
+        floor_raw = [load_weight("floor", floor_w, 0, "table0"), load_weight("floor", floor_w, 1, "fam0_then_floor1")]
+        nc.vector.tensor_copy(cand_v[1][:], tab_w[1][:].indirect(cand_list[:]))
+        nc.vector.tensor_copy(fam_v[1][:], tab_w[1][:].indirect(fam_list[:]))
+        nc.vector.tensor_copy(cand_sc[1][:], tab_sc_last[:].indirect(cand_list[:]))
+
+        fam_q = [quantise_weight("fam0", fam_bf[0])]
+        fam_bf.append(round_weight(1, fam_raw[1], nc.vector.tensor_copy))
+        fam_q.append(quantise_weight("fam1", fam_bf[1]))
+        slot_w = held("slot_w", [P, N], U32, "first_scales_then_fam1")
+        nc.sync.dma_start(slot_w[:].bitcast(I32), slot_w_words[0].rearrange("p c i -> p (c i)").bitcast(I32))
+        floor_bf = [round_weight(0, floor_raw[0], nc.vector.tensor_copy)]
+        floor_q = [quantise_weight("floor0", floor_bf[0])]
+        floor_bf.append(round_weight(1, floor_raw[1], nc.vector.tensor_copy))
+        floor_q.append(quantise_weight("floor1", floor_bf[1]))
+
+        half_d = keep.tile([P, ROW_TILES], F32, name="half_d")
+        nc.gpsimd.tensor_scalar(half_d[:], d_sb[:], 0.5, 0.0, ALU.mult, ALU.add)
+
+        identity = held("identity", [P, P], F32)
+        make_identity(nc, identity[:])
+
+        def first_product(tag, c, stationary, moving):
+            acc = psum.tile([P, PACK, CHUNK], F32, name=tag, tag=tag)
+            for a in range(PASSES):
+                rhs, rhs_scale = moving(a, slice(c * CHUNK, (c + 1) * CHUNK))
+                for t in range(PACK):
+                    lhsT, lhsT_scale = stationary(a, t)
+                    nc.tensor.matmul_mx(
+                        acc[:, t, :], lhsT=lhsT, lhsT_scale=lhsT_scale, rhs=rhs, rhs_scale=rhs_scale,
+                        start=(a == 0 and t == 0), stop=(a == PASSES - 1 and t == PACK - 1),
+                    )
+            return acc
+
+        def quantised_columns(planes):
+            def pick(a, t):
+                codes, scales = planes[a]
+                return codes[:, t * P : (t + 1) * P].bitcast(FP8X4), scales[:, t * P : (t + 1) * P]
+            return pick
+
+        def fam_tokens(a, cols):
+            return fam_v[a][:, cols].bitcast(FP8X4), fam_sc[4 * a : P, cols]
+
+        h_codes = held("h_codes", [P, S], U32)
+        h_scales = held("h_scales", [P, S], U8)
+
+        def cand_tanh(c):
+            cols = slice(c * CHUNK, (c + 1) * CHUNK)
+            cand = psum.tile([CHUNK, H], F32, name="cand", tag="cand_then_low")
+            for a in range(PASSES):
+                nc.tensor.matmul_mx(
+                    cand[:], lhsT=cand_v[a][:, cols].bitcast(FP8X4), lhsT_scale=cand_sc[a][:, cols],
+                    rhs=cand_w[:, a, :].bitcast(FP4X4), rhs_scale=cand_w_sc[:, a, :],
+                    start=(a == 0), stop=(a == PASSES - 1),
+                )
+            tanh_rows = held("tanh_rows%d" % c, [CHUNK, PACK, P], F32)
+            nc.scalar.activation(tanh_rows[:], cand[:].rearrange("j (m t) -> j t m", t=PACK), ACT.Tanh)
+            return tanh_rows
+
+        def features(c, tanh_rows):
+            cols = slice(c * CHUNK, (c + 1) * CHUNK)
+            tanh_c = psum.tile([P, PACK, CHUNK], F32, name="tanh_c")
+            for t in range(PACK):
+                nc.tensor.transpose(tanh_c[:, t, :], tanh_rows[:, t, :], identity[:])
+            fam = first_product("fam", c, quantised_columns(fam_q), fam_tokens)
+            fold1 = ring.tile([P, PACK, CHUNK], F32, name="fold1")
+            nc.scalar.activation(fold1[:], fam[:], ACT.Abs, bias=-math.pi / 2)
+            fold2 = ring.tile([P, PACK, CHUNK], F32, name="fold2")
+            nc.scalar.activation(fold2[:], fold1[:], ACT.Abs, scale=-1.0, bias=math.pi)
+            sin_f = ring.tile([P, PACK, CHUNK], F32, name="sin_f", bufs=CHUNKS)
+            nc.scalar.activation(sin_f[:], fold2[:], ACT.Sin, bias=-math.pi / 2)
+            prod = keep.tile([P, PACK, CHUNK], F32, name="prod", tag="scratch1", align_bytes=64)
+            for t in range(PACK):
+                nc.vector.scalar_tensor_tensor(
+                    prod[:, t, :], sin_f[:, t, :], gain_sb[:, t : t + 1], tanh_c[:, t, :], ALU.mult, ALU.mult
+                )
+            low = first_product("cand_then_low", c, quantised_columns(floor_q), fam_tokens)
+            h_bf = keep.tile([P, CHUNK, PACK], BF16, name="h_bf", tag="scratch0", align_bytes=64)
+            nc.vector.tensor_tensor(
+                h_bf[:].rearrange("p (g i) t -> p g t i", i=4),
+                prod[:].rearrange("p t (g i) -> p g t i", i=4),
+                low[:].rearrange("p t (g i) -> p g t i", i=4),
+                ALU.max,
+            )
+            nc.vector.quantize_mx(
+                h_codes[:, cols].bitcast(FP8X4), h_scales[:, cols], h_bf[:].rearrange("p n t -> p (n t)")
+            )
+
+        def place(n, first, widths):
+            width = sum(widths)
+            rows = slice(n * P, (n + 1) * P)
+            acc = psum.tile([P, S], F32, name="e", tag="e")
+            at = first
+            for w in widths:
+                nc.tensor.matmul_mx(
+                    acc[:, at : at + w], lhsT=slot_w[:, rows].bitcast(FP8X4), lhsT_scale=slot_sc[:, rows],
+                    rhs=h_codes[:, at : at + w].bitcast(FP8X4), rhs_scale=h_scales[:, at : at + w],
+                    start=True, stop=True,
+                )
+                at = at + w
+            cols = slice(first, first + width)
+            th = ring.tile([P, S], F32, name="th")
+            nc.scalar.activation(th[:, cols], acc[:, cols], ACT.Tanh, scale=0.5, bias=half_d[:, n : n + 1])
+            y = ring.tile([P, S], F32, name="y")
+            nc.scalar.activation(y[:, cols], th[:, cols], ACT.Copy, scale=0.5, bias=0.5)
+            page = pages[n % PAGES]
+            nc.vector.tensor_tensor(
+                page[:].indirect(slot_list[:, first // 16 : (first + width) // 16]),
+                y[:, cols], wgo_sb[:, cols], ALU.mult,
+            )
+            if first + width == S:
+                nc.sync.dma_start(out[rows, :], page[:])
+
+        placed = [1, 1, 2, 3]
+        tanhs = [cand_tanh(c) for c in range(CHUNKS)]
+        wgo_sb = held("wgo_sb", [P, S], F32, "cand_w_then_wgo")
+        nc.sync.dma_start(wgo_sb[:], wgo)
+        slot_sc = held("slot_sc", [P, N], U8, "weight_scales")
+        nc.gpsimd.memset(slot_sc[:].bitcast(I32), 0)
+        slot_sc_hbm = slot_w_scales.bitcast(I32)
+        for q in range(QUADS):
+            nc.sync.dma_start(slot_sc[quad_rows(q, 0, 4), :].bitcast(I32), slot_sc_hbm[0, 4 * q : 4 * q + 4, :])
+        features(0, tanhs[0])
+        for c in range(1, CHUNKS):
+            features(c, tanhs[c])
+            for n in range(PAGES):
+                if placed[n] == c:
+                    place(n, 0, [CHUNK] * c)
+        for n in range(PAGES):
+            place(n, placed[n] * CHUNK, [CHUNK] * (CHUNKS - placed[n]))
+        for n in range(PAGES, ROW_TILES):
+            place(n, 0, [S])

@@ -24,8 +24,9 @@ PASSES = K // (P * PACK)
 QUADS = 4
 CHUNK = 128
 CHUNKS = S // CHUNK
+HALF = S // 2
 ROW_TILES = N // P
-PAGES = 4
+PAGES = 3
 
 
 def tile_list_host_family_slots_kernel(
@@ -44,15 +45,13 @@ def tile_list_host_family_slots_kernel(
         def quad_rows(q, first, count):
             return slice(32 * q + first, 32 * q + first + count)
 
-        tab_sc_both = held("tab_sc_both", [P, T], U8, "first_scales_then_fam1")
+        tab_sc_both = held("tab_sc_both", [P, T], U8, "scales_table1_floor1")
         tab_sc_last = held("tab_sc_last", [P, T], U8, "scratch1")
         cand_w_sc = held("cand_w_sc", [P, PASSES, H], U8, "weight_scales")
         nc.vector.memset(tab_sc_both[:].bitcast(I32), 0)
         nc.vector.memset(tab_sc_last[:].bitcast(I32), 0)
         nc.vector.memset(cand_w_sc[:].bitcast(I32), 0)
         pages = [held("page%d" % i, [P, T2], F32) for i in range(PAGES)]
-        for page in pages[:2]:
-            nc.gpsimd.memset(page[:].bitcast(I32), 0)
 
         fam_list = keep.tile([P, S // 16], U16, name="fam_list")
         cand_list = keep.tile([P, S // 16], U16, name="cand_list")
@@ -63,16 +62,15 @@ def tile_list_host_family_slots_kernel(
             nc.sync.dma_start(raw[:], w[a * P * PACK : (a + 1) * P * PACK, :].rearrange("(p j) c -> p j c", j=PACK))
             return raw
 
-        def load_table(a):
-            words = held("tab_w%d" % a, [P, T], U32, "table%d" % a)
+        def load_table(a, tag):
+            words = held("tab_w%d" % a, [P, T], U32, tag)
             nc.sync.dma_start(words[:].bitcast(I32), tab_words[a].rearrange("p t i -> p (t i)").bitcast(I32))
             return words
 
         nc.sync.dma_start(cand_list[:], offs2)
         nc.sync.dma_start(fam_list[:], offs)
-        tab_w = [load_table(0)]
-        fam_raw = [load_weight("fam", fam_w, 0, "fam0_then_floor1")]
-        tab_w.append(load_table(1))
+        tab_w = [load_table(0, "table0_fam1_slot")]
+        fam_raw = [load_weight("fam", fam_w, 0, "fam0_floor0")]
         cand_w = held("cand_w", [P, PASSES, 2 * H], U8, "cand_w_then_wgo")
         nc.sync.dma_start(cand_w[:].bitcast(I32), cand_w_words.bitcast(I32).rearrange("a p b -> p a b"))
         nc.sync.dma_start(slot_list[:], offs3)
@@ -87,19 +85,17 @@ def tile_list_host_family_slots_kernel(
                 cand_w_sc[quad_rows(q, 0, 4), :, :].bitcast(I32),
                 cand_sc_hbm[:, 4 * q : 4 * q + 4, :].rearrange("a r c -> r a c"),
             )
-        gain_sb = keep.tile([P, PACK], F32, name="gain_sb")
-        nc.gpsimd.dma_start(gain_sb[:], gain.rearrange("(p t) -> p t", t=PACK))
-        d_sb = keep.tile([P, ROW_TILES], F32, name="d_sb")
-        with nc.allow_non_contiguous_dma(reason="one bias value to a partition"):
-            nc.gpsimd.dma_start(d_sb[:], d.rearrange("(c p) -> p c", p=P))
-
+        warm = keep.tile([P, 1], F32, name="warm")
+        nc.vector.memset(warm[:], 0.0)
+        warm_out = keep.tile([P, 1], F32, name="warm_out")
+        nc.scalar.activation(warm_out[:], warm[:], ACT.Silu)
 
         fam_sc = held("fam_sc", [P, S], U8)
-        cand_sc = [held("cand_sc%d" % a, [P, S], U8) for a in range(PASSES)]
+        cand_sc = [held("cand_sc%d" % a, [P, S], U8, "cand_sc%d" % a) for a in range(PASSES)]
         nc.vector.tensor_copy(fam_sc[:], tab_sc_both[:].indirect(fam_list[:]))
         nc.vector.tensor_copy(cand_sc[0][:], tab_sc_both[:].indirect(cand_list[:]))
-        fam_raw.append(load_weight("fam", fam_w, 1, "first_scales_then_fam1"))
-        for page in pages[2:]:
+        tab_w.append(load_table(1, "scales_table1_floor1"))
+        for page in pages:
             nc.vector.memset(page[:].bitcast(I32), 0)
 
         def round_weight(a, raw, copy):
@@ -119,50 +115,36 @@ def tile_list_host_family_slots_kernel(
         cand_v = [held("cand_v%d" % a, [P, S], U32) for a in range(PASSES)]
         nc.vector.tensor_copy(cand_v[0][:], tab_w[0][:].indirect(cand_list[:]))
         nc.vector.tensor_copy(fam_v[0][:], tab_w[0][:].indirect(fam_list[:]))
-        floor_raw = [load_weight("floor", floor_w, 0, "table0"), load_weight("floor", floor_w, 1, "fam0_then_floor1")]
+        fam_raw.append(load_weight("fam", fam_w, 1, "table0_fam1_slot"))
+        floor_raw = [load_weight("floor", floor_w, 0, "fam0_floor0")]
         nc.vector.tensor_copy(cand_v[1][:], tab_w[1][:].indirect(cand_list[:]))
         nc.vector.tensor_copy(fam_v[1][:], tab_w[1][:].indirect(fam_list[:]))
         nc.vector.tensor_copy(cand_sc[1][:], tab_sc_last[:].indirect(cand_list[:]))
 
+        floor_raw.append(load_weight("floor", floor_w, 1, "scales_table1_floor1"))
         fam_q = [quantise_weight("fam0", fam_bf[0])]
         fam_bf.append(round_weight(1, fam_raw[1], nc.vector.tensor_copy))
         fam_q.append(quantise_weight("fam1", fam_bf[1]))
-        slot_w = held("slot_w", [P, N], U32, "first_scales_then_fam1")
+        slot_w = held("slot_w", [P, N], U32, "table0_fam1_slot")
         nc.sync.dma_start(slot_w[:].bitcast(I32), slot_w_words[0].rearrange("p c i -> p (c i)").bitcast(I32))
         floor_bf = [round_weight(0, floor_raw[0], nc.vector.tensor_copy)]
         floor_q = [quantise_weight("floor0", floor_bf[0])]
         floor_bf.append(round_weight(1, floor_raw[1], nc.vector.tensor_copy))
         floor_q.append(quantise_weight("floor1", floor_bf[1]))
 
-        half_d = keep.tile([P, ROW_TILES], F32, name="half_d")
-        nc.gpsimd.tensor_scalar(half_d[:], d_sb[:], 0.5, 0.0, ALU.mult, ALU.add)
-
         identity = held("identity", [P, P], F32)
         make_identity(nc, identity[:])
 
-        def first_product(tag, c, stationary, moving):
-            acc = psum.tile([P, PACK, CHUNK], F32, name=tag, tag=tag)
+        def family_product(acc, planes, ts, cols):
             for a in range(PASSES):
-                rhs, rhs_scale = moving(a, slice(c * CHUNK, (c + 1) * CHUNK))
-                for t in range(PACK):
-                    lhsT, lhsT_scale = stationary(a, t)
-                    nc.tensor.matmul_mx(
-                        acc[:, t, :], lhsT=lhsT, lhsT_scale=lhsT_scale, rhs=rhs, rhs_scale=rhs_scale,
-                        start=(a == 0 and t == 0), stop=(a == PASSES - 1 and t == PACK - 1),
-                    )
-            return acc
-
-        def quantised_columns(planes):
-            def pick(a, t):
                 codes, scales = planes[a]
-                return codes[:, t * P : (t + 1) * P].bitcast(FP8X4), scales[:, t * P : (t + 1) * P]
-            return pick
-
-        def fam_tokens(a, cols):
-            return fam_v[a][:, cols].bitcast(FP8X4), fam_sc[4 * a : P, cols]
-
-        h_codes = held("h_codes", [P, S], U32)
-        h_scales = held("h_scales", [P, S], U8)
+                for i, t in enumerate(ts):
+                    nc.tensor.matmul_mx(
+                        acc[:, i, :],
+                        lhsT=codes[:, t * P : (t + 1) * P].bitcast(FP8X4), lhsT_scale=scales[:, t * P : (t + 1) * P],
+                        rhs=fam_v[a][:, cols].bitcast(FP8X4), rhs_scale=fam_sc[4 * a : P, cols],
+                        start=(a == 0 and i == 0), stop=(a == PASSES - 1 and i == len(ts) - 1),
+                    )
 
         def cand_tanh(c):
             cols = slice(c * CHUNK, (c + 1) * CHUNK)
@@ -177,31 +159,49 @@ def tile_list_host_family_slots_kernel(
             nc.scalar.activation(tanh_rows[:], cand[:].rearrange("j (m t) -> j t m", t=PACK), ACT.Tanh)
             return tanh_rows
 
-        def features(c, tanh_rows):
-            cols = slice(c * CHUNK, (c + 1) * CHUNK)
-            tanh_c = psum.tile([P, PACK, CHUNK], F32, name="tanh_c")
-            for t in range(PACK):
-                nc.tensor.transpose(tanh_c[:, t, :], tanh_rows[:, t, :], identity[:])
-            fam = first_product("fam", c, quantised_columns(fam_q), fam_tokens)
-            fold1 = ring.tile([P, PACK, CHUNK], F32, name="fold1")
-            nc.scalar.activation(fold1[:], fam[:], ACT.Abs, bias=-math.pi / 2)
-            fold2 = ring.tile([P, PACK, CHUNK], F32, name="fold2")
+        h_codes = held("h_codes", [P, S], U32)
+        h_scales = held("h_scales", [P, S], U8)
+
+        def product_term(half, tanh_rows):
+            cols = slice(half * HALF, (half + 1) * HALF)
+            fold1 = ring.tile([P, PACK, HALF], F32, name="fold1")
+            for t0 in (0, 2):
+                fam = psum.tile([P, 2, HALF], F32, name="fam")
+                family_product(fam, fam_q, (t0, t0 + 1), cols)
+                nc.scalar.activation(fold1[:, t0 : t0 + 2, :], fam[:], ACT.Abs, bias=-math.pi / 2)
+            fold2 = ring.tile([P, PACK, HALF], F32, name="fold2")
             nc.scalar.activation(fold2[:], fold1[:], ACT.Abs, scale=-1.0, bias=math.pi)
-            sin_f = ring.tile([P, PACK, CHUNK], F32, name="sin_f", bufs=CHUNKS)
+            sin_f = ring.tile([P, PACK, HALF], F32, name="sin_f")
             nc.scalar.activation(sin_f[:], fold2[:], ACT.Sin, bias=-math.pi / 2)
-            prod = keep.tile([P, PACK, CHUNK], F32, name="prod", tag="scratch1", align_bytes=64)
-            for t in range(PACK):
-                nc.vector.scalar_tensor_tensor(
-                    prod[:, t, :], sin_f[:, t, :], gain_sb[:, t : t + 1], tanh_c[:, t, :], ALU.mult, ALU.mult
+            prod = held("prod", [P, PACK, HALF], F32, "scratch1")
+            for t0 in (0, 2):
+                tanh_c = psum.tile([P, 2, HALF], F32, name="tanh_c")
+                for i in range(2):
+                    for c in range(2):
+                        nc.tensor.transpose(
+                            tanh_c[:, i, c * CHUNK : (c + 1) * CHUNK], tanh_rows[c][:, t0 + i, :], identity[:]
+                        )
+                for i in range(2):
+                    t = t0 + i
+                    nc.vector.scalar_tensor_tensor(
+                        prod[:, t, :], sin_f[:, t, :], gain_sb[:, t : t + 1], tanh_c[:, i, :], ALU.mult, ALU.mult
+                    )
+            return prod
+
+        def features(half, prod):
+            h_bf = held("h_bf", [P, HALF, PACK], BF16, "scratch0")
+            for c in range(2):
+                first = half * HALF + c * CHUNK
+                low = psum.tile([P, PACK, CHUNK], F32, name="low", tag="cand_then_low")
+                family_product(low, floor_q, range(PACK), slice(first, first + CHUNK))
+                inner = slice(c * CHUNK, (c + 1) * CHUNK)
+                nc.vector.tensor_tensor(
+                    h_bf[:, inner, :].rearrange("p (g i) t -> p g t i", i=4),
+                    prod[:, :, inner].rearrange("p t (g i) -> p g t i", i=4),
+                    low[:].rearrange("p t (g i) -> p g t i", i=4),
+                    ALU.max,
                 )
-            low = first_product("cand_then_low", c, quantised_columns(floor_q), fam_tokens)
-            h_bf = keep.tile([P, CHUNK, PACK], BF16, name="h_bf", tag="scratch0", align_bytes=64)
-            nc.vector.tensor_tensor(
-                h_bf[:].rearrange("p (g i) t -> p g t i", i=4),
-                prod[:].rearrange("p t (g i) -> p g t i", i=4),
-                low[:].rearrange("p t (g i) -> p g t i", i=4),
-                ALU.max,
-            )
+            cols = slice(half * HALF, (half + 1) * HALF)
             nc.vector.quantize_mx(
                 h_codes[:, cols].bitcast(FP8X4), h_scales[:, cols], h_bf[:].rearrange("p n t -> p (n t)")
             )
@@ -231,22 +231,27 @@ def tile_list_host_family_slots_kernel(
             if first + width == S:
                 nc.sync.dma_start(out[rows, :], page[:])
 
-        placed = [1, 1, 2, 3]
         tanhs = [cand_tanh(c) for c in range(CHUNKS)]
+        gain_sb = held("gain_sb", [P, PACK], F32, "cand_sc0")
+        nc.sync.dma_start(gain_sb[:], gain.rearrange("(p t) -> p t", t=PACK))
+        d_sb = held("d_sb", [P, ROW_TILES], F32, "cand_sc1")
+        with nc.allow_non_contiguous_dma(reason="one bias value to a partition"):
+            nc.sync.dma_start(d_sb[:], d.rearrange("(c p) -> p c", p=P))
+        half_d = keep.tile([P, ROW_TILES], F32, name="half_d")
+        nc.vector.tensor_scalar(half_d[:], d_sb[:], 0.5, 0.0, ALU.mult, ALU.add)
         wgo_sb = held("wgo_sb", [P, S], F32, "cand_w_then_wgo")
         nc.sync.dma_start(wgo_sb[:], wgo)
         slot_sc = held("slot_sc", [P, N], U8, "weight_scales")
-        nc.gpsimd.memset(slot_sc[:].bitcast(I32), 0)
+        nc.vector.memset(slot_sc[:].bitcast(I32), 0)
         slot_sc_hbm = slot_w_scales.bitcast(I32)
         for q in range(QUADS):
             nc.sync.dma_start(slot_sc[quad_rows(q, 0, 4), :].bitcast(I32), slot_sc_hbm[0, 4 * q : 4 * q + 4, :])
-        features(0, tanhs[0])
-        for c in range(1, CHUNKS):
-            features(c, tanhs[c])
-            for n in range(PAGES):
-                if placed[n] == c:
-                    place(n, 0, [CHUNK] * c)
-        for n in range(PAGES):
-            place(n, placed[n] * CHUNK, [CHUNK] * (CHUNKS - placed[n]))
-        for n in range(PAGES, ROW_TILES):
+        features(0, product_term(0, tanhs[:2]))
+        second = product_term(1, tanhs[2:])
+        place(0, 0, [HALF])
+        features(1, second)
+        place(1, 0, [HALF])
+        place(0, HALF, [HALF])
+        place(1, HALF, [HALF])
+        for n in range(2, ROW_TILES):
             place(n, 0, [S])

@@ -45,62 +45,80 @@ def tile_list_host_family_slots_kernel(
         def quad_rows(q, first, count):
             return slice(32 * q + first, 32 * q + first + count)
 
-        tab_sc_both = held("tab_sc_both", [P, T], U8, "scales_table1_floor1")
+        tab_sc_both = held("tab_sc_both", [P, T], U8)
+        cand_w_sc = held("cand_w_sc", [P, PASSES, H], U8)
         tab_sc_last = held("tab_sc_last", [P, T], U8, "scratch1")
-        cand_w_sc = held("cand_w_sc", [P, PASSES, H], U8, "weight_scales")
-        nc.vector.memset(tab_sc_both[:].bitcast(I32), 0)
-        nc.vector.memset(tab_sc_last[:].bitcast(I32), 0)
-        nc.vector.memset(cand_w_sc[:].bitcast(I32), 0)
+        slot_sc = held("slot_sc", [P, N], U8)
+        for plane in (tab_sc_both, cand_w_sc, tab_sc_last, slot_sc):
+            nc.vector.memset(plane[:].bitcast(I32), 0)
         pages = [held("page%d" % i, [P, T2], F32) for i in range(PAGES)]
 
         fam_list = keep.tile([P, S // 16], U16, name="fam_list")
         cand_list = keep.tile([P, S // 16], U16, name="cand_list")
         slot_list = keep.tile([P, S // 16], U16, name="slot_list")
+        nc.sync.dma_start(cand_list[:], offs2)
+        nc.sync.dma_start(fam_list[:], offs)
+        nc.sync.dma_start(slot_list[:], offs3)
+        gain_sb = held("gain_sb", [P, PACK], F32)
+        nc.sync.dma_start(gain_sb[:], gain.rearrange("(p t) -> p t", t=PACK))
 
-        def load_weight(name, w, a, tag):
-            raw = held("%s_raw%d" % (name, a), [P, PACK, H], F32, tag)
+        def load_weight(name, w, a):
+            raw = held("%s_raw%d" % (name, a), [P, PACK, H], F32)
             nc.sync.dma_start(raw[:], w[a * P * PACK : (a + 1) * P * PACK, :].rearrange("(p j) c -> p j c", j=PACK))
             return raw
 
-        def load_table(a, tag):
-            words = held("tab_w%d" % a, [P, T], U32, tag)
-            nc.sync.dma_start(words[:].bitcast(I32), tab_words[a].rearrange("p t i -> p (t i)").bitcast(I32))
+        def load_table(a, pieces):
+            words = held("tab_w%d" % a, [P, T], U32)
+            source = tab_words[a].rearrange("p t i -> p (t i)").bitcast(I32)
+            for i in range(pieces):
+                cols = slice(i * T // pieces, (i + 1) * T // pieces)
+                nc.sync.dma_start(words[:, cols].bitcast(I32), source[:, cols])
             return words
 
-        nc.sync.dma_start(cand_list[:], offs2)
-        nc.sync.dma_start(fam_list[:], offs)
-        tab_w = [load_table(0, "table0_fam1_slot")]
-        fam_raw = [load_weight("fam", fam_w, 0, "fam0_floor0")]
-        cand_w = held("cand_w", [P, PASSES, 2 * H], U8, "cand_w_then_wgo")
-        nc.sync.dma_start(cand_w[:].bitcast(I32), cand_w_words.bitcast(I32).rearrange("a p b -> p a b"))
-        nc.sync.dma_start(slot_list[:], offs3)
+        tab_w = [load_table(0, 4)]
         tab_sc_hbm = tab_scales.bitcast(I32)
         for q in range(QUADS):
-            nc.scalar.dma_start(tab_sc_both[quad_rows(q, 0, 8), :].bitcast(I32), tab_sc_hbm[:, 4 * q : 4 * q + 4, :])
-        for q in range(QUADS):
-            nc.scalar.dma_start(tab_sc_last[quad_rows(q, 0, 4), :].bitcast(I32), tab_sc_hbm[1, 4 * q : 4 * q + 4, :])
+            nc.sync.dma_start(tab_sc_both[quad_rows(q, 0, 8), :].bitcast(I32), tab_sc_hbm[:, 4 * q : 4 * q + 4, :])
+        fam_raw = [load_weight("fam", fam_w, 0)]
         cand_sc_hbm = cand_w_scales.bitcast(I32)
         for q in range(QUADS):
-            nc.scalar.dma_start(
+            nc.sync.dma_start(
                 cand_w_sc[quad_rows(q, 0, 4), :, :].bitcast(I32),
                 cand_sc_hbm[:, 4 * q : 4 * q + 4, :].rearrange("a r c -> r a c"),
             )
+        for q in range(QUADS):
+            nc.sync.dma_start(tab_sc_last[quad_rows(q, 0, 4), :].bitcast(I32), tab_sc_hbm[1, 4 * q : 4 * q + 4, :])
+        cand_w = held("cand_w", [P, PASSES, 2 * H], U8)
+        nc.sync.dma_start(cand_w[:].bitcast(I32), cand_w_words.bitcast(I32).rearrange("a p b -> p a b"))
+        tab_w.append(load_table(1, 1))
+        fam_raw.append(load_weight("fam", fam_w, 1))
+        floor_raw = [load_weight("floor", floor_w, a) for a in range(PASSES)]
+        d_sb = held("d_sb", [P, ROW_TILES], F32)
+        with nc.allow_non_contiguous_dma(reason="one bias value to a partition"):
+            nc.sync.dma_start(d_sb[:], d.rearrange("(c p) -> p c", p=P))
+        slot_w = held("slot_w", [P, N], U32)
+        nc.sync.dma_start(slot_w[:].bitcast(I32), slot_w_words[0].rearrange("p c i -> p (c i)").bitcast(I32))
+        slot_sc_hbm = slot_w_scales.bitcast(I32)
+        for q in range(QUADS):
+            nc.sync.dma_start(slot_sc[quad_rows(q, 0, 4), :].bitcast(I32), slot_sc_hbm[0, 4 * q : 4 * q + 4, :])
+        wgo_sb = held("wgo_sb", [P, S], F32)
+        nc.sync.dma_start(wgo_sb[:], wgo)
+
         warm = keep.tile([P, 1], F32, name="warm")
         nc.vector.memset(warm[:], 0.0)
         warm_out = keep.tile([P, 1], F32, name="warm_out")
         nc.scalar.activation(warm_out[:], warm[:], ACT.Silu)
 
         fam_sc = held("fam_sc", [P, S], U8)
-        cand_sc = [held("cand_sc%d" % a, [P, S], U8, "cand_sc%d" % a) for a in range(PASSES)]
+        cand_sc = [held("cand_sc%d" % a, [P, S], U8) for a in range(PASSES)]
         nc.vector.tensor_copy(fam_sc[:], tab_sc_both[:].indirect(fam_list[:]))
         nc.vector.tensor_copy(cand_sc[0][:], tab_sc_both[:].indirect(cand_list[:]))
-        tab_w.append(load_table(1, "scales_table1_floor1"))
         for page in pages:
-            nc.vector.memset(page[:].bitcast(I32), 0)
+            nc.gpsimd.memset(page[:].bitcast(I32), 0)
 
         def round_weight(a, raw, copy):
             rounded = held("rounded%d" % a, [P, PACK, P, PACK], BF16, "scratch%d" % a)
-            copy(rounded[:].rearrange("p t m j -> p m j t"), raw[:].rearrange("p j (m t) -> p m j t", t=PACK))
+            copy(rounded[:].rearrange("p t m j -> p m t j"), raw[:].rearrange("p j (m t) -> p m t j", t=PACK))
             return rounded
 
         def quantise_weight(name, rounded):
@@ -115,18 +133,13 @@ def tile_list_host_family_slots_kernel(
         cand_v = [held("cand_v%d" % a, [P, S], U32) for a in range(PASSES)]
         nc.vector.tensor_copy(cand_v[0][:], tab_w[0][:].indirect(cand_list[:]))
         nc.vector.tensor_copy(fam_v[0][:], tab_w[0][:].indirect(fam_list[:]))
-        fam_raw.append(load_weight("fam", fam_w, 1, "table0_fam1_slot"))
-        floor_raw = [load_weight("floor", floor_w, 0, "fam0_floor0")]
+        nc.vector.tensor_copy(cand_sc[1][:], tab_sc_last[:].indirect(cand_list[:]))
         nc.vector.tensor_copy(cand_v[1][:], tab_w[1][:].indirect(cand_list[:]))
         nc.vector.tensor_copy(fam_v[1][:], tab_w[1][:].indirect(fam_list[:]))
-        nc.vector.tensor_copy(cand_sc[1][:], tab_sc_last[:].indirect(cand_list[:]))
 
-        floor_raw.append(load_weight("floor", floor_w, 1, "scales_table1_floor1"))
         fam_q = [quantise_weight("fam0", fam_bf[0])]
         fam_bf.append(round_weight(1, fam_raw[1], nc.vector.tensor_copy))
         fam_q.append(quantise_weight("fam1", fam_bf[1]))
-        slot_w = held("slot_w", [P, N], U32, "table0_fam1_slot")
-        nc.sync.dma_start(slot_w[:].bitcast(I32), slot_w_words[0].rearrange("p c i -> p (c i)").bitcast(I32))
         floor_bf = [round_weight(0, floor_raw[0], nc.vector.tensor_copy)]
         floor_q = [quantise_weight("floor0", floor_bf[0])]
         floor_bf.append(round_weight(1, floor_raw[1], nc.vector.tensor_copy))
@@ -231,23 +244,12 @@ def tile_list_host_family_slots_kernel(
             if first + width == S:
                 nc.sync.dma_start(out[rows, :], page[:])
 
-        tanhs = [cand_tanh(c) for c in range(CHUNKS)]
-        gain_sb = held("gain_sb", [P, PACK], F32, "cand_sc0")
-        nc.sync.dma_start(gain_sb[:], gain.rearrange("(p t) -> p t", t=PACK))
-        d_sb = held("d_sb", [P, ROW_TILES], F32, "cand_sc1")
-        with nc.allow_non_contiguous_dma(reason="one bias value to a partition"):
-            nc.sync.dma_start(d_sb[:], d.rearrange("(c p) -> p c", p=P))
         half_d = keep.tile([P, ROW_TILES], F32, name="half_d")
         nc.vector.tensor_scalar(half_d[:], d_sb[:], 0.5, 0.0, ALU.mult, ALU.add)
-        wgo_sb = held("wgo_sb", [P, S], F32, "cand_w_then_wgo")
-        nc.sync.dma_start(wgo_sb[:], wgo)
-        slot_sc = held("slot_sc", [P, N], U8, "weight_scales")
-        nc.vector.memset(slot_sc[:].bitcast(I32), 0)
-        slot_sc_hbm = slot_w_scales.bitcast(I32)
-        for q in range(QUADS):
-            nc.sync.dma_start(slot_sc[quad_rows(q, 0, 4), :].bitcast(I32), slot_sc_hbm[0, 4 * q : 4 * q + 4, :])
-        features(0, product_term(0, tanhs[:2]))
-        second = product_term(1, tanhs[2:])
+        first = product_term(0, [cand_tanh(0), cand_tanh(1)])
+        later_tanh = [cand_tanh(2), cand_tanh(3)]
+        features(0, first)
+        second = product_term(1, later_tanh)
         place(0, 0, [HALF])
         features(1, second)
         place(1, 0, [HALF])

@@ -49,7 +49,7 @@ def tile_list_host_family_slots_kernel(
         cand_w_sc = held("cand_w_sc", [P, PASSES, H], U8)
         tab_sc_last = held("tab_sc_last", [P, T], U8, "scratch1")
         slot_sc = held("slot_sc", [P, N], U8)
-        for plane in (tab_sc_both, cand_w_sc, tab_sc_last, slot_sc):
+        for plane in (tab_sc_both, tab_sc_last, cand_w_sc, slot_sc):
             nc.vector.memset(plane[:].bitcast(I32), 0)
         pages = [held("page%d" % i, [P, T2], F32) for i in range(PAGES)]
 
@@ -67,31 +67,27 @@ def tile_list_host_family_slots_kernel(
             nc.sync.dma_start(raw[:], w[a * P * PACK : (a + 1) * P * PACK, :].rearrange("(p j) c -> p j c", j=PACK))
             return raw
 
-        def load_table(a, pieces):
+        def load_table(a):
             words = held("tab_w%d" % a, [P, T], U32)
-            source = tab_words[a].rearrange("p t i -> p (t i)").bitcast(I32)
-            for i in range(pieces):
-                cols = slice(i * T // pieces, (i + 1) * T // pieces)
-                nc.sync.dma_start(words[:, cols].bitcast(I32), source[:, cols])
+            nc.sync.dma_start(words[:].bitcast(I32), tab_words[a].rearrange("p t i -> p (t i)").bitcast(I32))
             return words
 
-        tab_w = [load_table(0, 4)]
+        tab_w = [load_table(a) for a in range(PASSES)]
+        fam_raw = [load_weight("fam", fam_w, 0)]
+        cand_w = held("cand_w", [P, PASSES, 2 * H], U8)
+        nc.sync.dma_start(cand_w[:].bitcast(I32), cand_w_words.bitcast(I32).rearrange("a p b -> p a b"))
         tab_sc_hbm = tab_scales.bitcast(I32)
         for q in range(QUADS):
             nc.sync.dma_start(tab_sc_both[quad_rows(q, 0, 8), :].bitcast(I32), tab_sc_hbm[:, 4 * q : 4 * q + 4, :])
-        fam_raw = [load_weight("fam", fam_w, 0)]
+        fam_raw.append(load_weight("fam", fam_w, 1))
+        for q in range(QUADS):
+            nc.sync.dma_start(tab_sc_last[quad_rows(q, 0, 4), :].bitcast(I32), tab_sc_hbm[1, 4 * q : 4 * q + 4, :])
         cand_sc_hbm = cand_w_scales.bitcast(I32)
         for q in range(QUADS):
             nc.sync.dma_start(
                 cand_w_sc[quad_rows(q, 0, 4), :, :].bitcast(I32),
                 cand_sc_hbm[:, 4 * q : 4 * q + 4, :].rearrange("a r c -> r a c"),
             )
-        for q in range(QUADS):
-            nc.sync.dma_start(tab_sc_last[quad_rows(q, 0, 4), :].bitcast(I32), tab_sc_hbm[1, 4 * q : 4 * q + 4, :])
-        cand_w = held("cand_w", [P, PASSES, 2 * H], U8)
-        nc.sync.dma_start(cand_w[:].bitcast(I32), cand_w_words.bitcast(I32).rearrange("a p b -> p a b"))
-        tab_w.append(load_table(1, 1))
-        fam_raw.append(load_weight("fam", fam_w, 1))
         floor_raw = [load_weight("floor", floor_w, a) for a in range(PASSES)]
         d_sb = held("d_sb", [P, ROW_TILES], F32)
         with nc.allow_non_contiguous_dma(reason="one bias value to a partition"):
@@ -109,10 +105,6 @@ def tile_list_host_family_slots_kernel(
         warm_out = keep.tile([P, 1], F32, name="warm_out")
         nc.scalar.activation(warm_out[:], warm[:], ACT.Silu)
 
-        fam_sc = held("fam_sc", [P, S], U8)
-        cand_sc = [held("cand_sc%d" % a, [P, S], U8) for a in range(PASSES)]
-        nc.vector.tensor_copy(fam_sc[:], tab_sc_both[:].indirect(fam_list[:]))
-        nc.vector.tensor_copy(cand_sc[0][:], tab_sc_both[:].indirect(cand_list[:]))
         for page in pages:
             nc.gpsimd.memset(page[:].bitcast(I32), 0)
 
@@ -131,11 +123,14 @@ def tile_list_host_family_slots_kernel(
 
         fam_v = [held("fam_v%d" % a, [P, S], U32) for a in range(PASSES)]
         cand_v = [held("cand_v%d" % a, [P, S], U32) for a in range(PASSES)]
-        nc.vector.tensor_copy(cand_v[0][:], tab_w[0][:].indirect(cand_list[:]))
-        nc.vector.tensor_copy(fam_v[0][:], tab_w[0][:].indirect(fam_list[:]))
+        for a in range(PASSES):
+            nc.vector.tensor_copy(cand_v[a][:], tab_w[a][:].indirect(cand_list[:]))
+            nc.vector.tensor_copy(fam_v[a][:], tab_w[a][:].indirect(fam_list[:]))
+        fam_sc = held("fam_sc", [P, S], U8)
+        cand_sc = [held("cand_sc%d" % a, [P, S], U8) for a in range(PASSES)]
+        nc.vector.tensor_copy(fam_sc[:], tab_sc_both[:].indirect(fam_list[:]))
+        nc.vector.tensor_copy(cand_sc[0][:], tab_sc_both[:].indirect(cand_list[:]))
         nc.vector.tensor_copy(cand_sc[1][:], tab_sc_last[:].indirect(cand_list[:]))
-        nc.vector.tensor_copy(cand_v[1][:], tab_w[1][:].indirect(cand_list[:]))
-        nc.vector.tensor_copy(fam_v[1][:], tab_w[1][:].indirect(fam_list[:]))
 
         fam_q = [quantise_weight("fam0", fam_bf[0])]
         fam_bf.append(round_weight(1, fam_raw[1], nc.vector.tensor_copy))
@@ -177,15 +172,14 @@ def tile_list_host_family_slots_kernel(
 
         def product_term(half, tanh_rows):
             cols = slice(half * HALF, (half + 1) * HALF)
-            fold1 = ring.tile([P, PACK, HALF], F32, name="fold1")
+            folded = held("folded", [P, PACK, HALF], F32)
             for t0 in (0, 2):
                 fam = psum.tile([P, 2, HALF], F32, name="fam")
                 family_product(fam, fam_q, (t0, t0 + 1), cols)
-                nc.scalar.activation(fold1[:, t0 : t0 + 2, :], fam[:], ACT.Abs, bias=-math.pi / 2)
-            fold2 = ring.tile([P, PACK, HALF], F32, name="fold2")
-            nc.scalar.activation(fold2[:], fold1[:], ACT.Abs, scale=-1.0, bias=math.pi)
+                nc.scalar.activation(folded[:, t0 : t0 + 2, :], fam[:], ACT.Abs, bias=-math.pi / 2)
+            nc.scalar.activation(folded[:], folded[:], ACT.Abs, scale=-1.0, bias=math.pi)
             sin_f = ring.tile([P, PACK, HALF], F32, name="sin_f")
-            nc.scalar.activation(sin_f[:], fold2[:], ACT.Sin, bias=-math.pi / 2)
+            nc.scalar.activation(sin_f[:], folded[:], ACT.Sin, bias=-math.pi / 2)
             prod = held("prod", [P, PACK, HALF], F32, "scratch1")
             for t0 in (0, 2):
                 tanh_c = psum.tile([P, 2, HALF], F32, name="tanh_c")
@@ -252,8 +246,9 @@ def tile_list_host_family_slots_kernel(
         second = product_term(1, later_tanh)
         place(0, 0, [HALF])
         features(1, second)
-        place(1, 0, [HALF])
-        place(0, HALF, [HALF])
-        place(1, HALF, [HALF])
-        for n in range(2, ROW_TILES):
+        for n in range(1, PAGES):
+            place(n, 0, [HALF])
+        for n in range(PAGES):
+            place(n, HALF, [HALF])
+        for n in range(PAGES, ROW_TILES):
             place(n, 0, [S])

import math
from contextlib import ExitStack

import concourse.mybir as mybir
from concourse.masks import make_identity

K, T, S, H, N, T2 = 1024, 2048, 512, 512, 768, 1024
FLOPS = 2 * S * (3 * K * H + H * N)

F32 = mybir.dt.float32
BF16 = mybir.dt.bfloat16
I32 = mybir.dt.int32
U32 = mybir.dt.uint32
U16 = mybir.dt.uint16
U8 = mybir.dt.uint8
FP8X4 = mybir.dt.float8_e4m3fn_x4
FP4X4 = mybir.dt.float4_e2m1fn_x4
ACT = mybir.ActivationFunctionType
ALU = mybir.AluOpType

P = 128
PACK = 4
PASSES = K // (P * PACK)
QUADS = 4
CHUNK = 128
CHUNKS = S // CHUNK
HALF = S // 2
ROW_TILES = N // P
PAGES = 3


def tile_list_host_family_slots_kernel(
    tc, tab_words, tab_scales, offs, offs2, offs3, fam_w, cand_w_words, cand_w_scales,
    floor_w, gain, slot_w_words, slot_w_scales, d, wgo, out,
):
    nc = tc.nc
    with ExitStack() as ctx:
        keep = ctx.enter_context(tc.tile_pool(name="keep", bufs=1))
        ring = ctx.enter_context(tc.tile_pool(name="ring", bufs=2))
        psum = ctx.enter_context(tc.psum_pool(name="psum", bufs=2))

        def held(name, shape, dtype, tag=""):
            return keep.tile(shape, dtype, name=name, tag=tag or name, align_bytes=64)

        def quad_rows(q, first, count):
            return slice(32 * q + first, 32 * q + first + count)

        tab_sc_both = held("tab_sc_both", [P, T], U8)
        cand_w_sc = held("cand_w_sc", [P, PASSES, H], U8)
        tab_sc_last = held("tab_sc_last", [P, T], U8, "scratch1")
        slot_sc = held("slot_sc", [P, N], U8)
        for plane in (tab_sc_both, tab_sc_last, cand_w_sc, slot_sc):
            nc.vector.memset(plane[:].bitcast(I32), 0)
        pages = [held("page%d" % i, [P, T2], F32) for i in range(PAGES)]

        fam_list = keep.tile([P, S // 16], U16, name="fam_list")
        cand_list = keep.tile([P, S // 16], U16, name="cand_list")
        slot_list = keep.tile([P, S // 16], U16, name="slot_list")
        nc.sync.dma_start(cand_list[:], offs2)
        nc.sync.dma_start(fam_list[:], offs)
        nc.sync.dma_start(slot_list[:], offs3)
        gain_sb = held("gain_sb", [P, PACK], F32)
        nc.sync.dma_start(gain_sb[:], gain.rearrange("(p t) -> p t", t=PACK))

        def load_weight(name, w, a):
            raw = held("%s_raw%d" % (name, a), [P, PACK, H], F32)
            nc.sync.dma_start(raw[:], w[a * P * PACK : (a + 1) * P * PACK, :].rearrange("(p j) c -> p j c", j=PACK))
            return raw

        def load_table(a):
            words = held("tab_w%d" % a, [P, T], U32)
            nc.sync.dma_start(words[:].bitcast(I32), tab_words[a].rearrange("p t i -> p (t i)").bitcast(I32))
            return words

        tab_w = [load_table(a) for a in range(PASSES)]
        fam_raw = [load_weight("fam", fam_w, 0)]
        cand_w = held("cand_w", [P, PASSES, 2 * H], U8)
        nc.sync.dma_start(cand_w[:].bitcast(I32), cand_w_words.bitcast(I32).rearrange("a p b -> p a b"))
        tab_sc_hbm = tab_scales.bitcast(I32)
        for q in range(QUADS):
            nc.sync.dma_start(tab_sc_both[quad_rows(q, 0, 8), :].bitcast(I32), tab_sc_hbm[:, 4 * q : 4 * q + 4, :])
        fam_raw.append(load_weight("fam", fam_w, 1))
        for q in range(QUADS):
            nc.sync.dma_start(tab_sc_last[quad_rows(q, 0, 4), :].bitcast(I32), tab_sc_hbm[1, 4 * q : 4 * q + 4, :])
        cand_sc_hbm = cand_w_scales.bitcast(I32)
        for q in range(QUADS):
            nc.sync.dma_start(
                cand_w_sc[quad_rows(q, 0, 4), :, :].bitcast(I32),
                cand_sc_hbm[:, 4 * q : 4 * q + 4, :].rearrange("a r c -> r a c"),
            )
        floor_raw = [load_weight("floor", floor_w, a) for a in range(PASSES)]
        d_sb = held("d_sb", [P, ROW_TILES], F32)
        with nc.allow_non_contiguous_dma(reason="one bias value to a partition"):
            nc.sync.dma_start(d_sb[:], d.rearrange("(c p) -> p c", p=P))
        slot_w = held("slot_w", [P, N], U32)
        nc.sync.dma_start(slot_w[:].bitcast(I32), slot_w_words[0].rearrange("p c i -> p (c i)").bitcast(I32))
        slot_sc_hbm = slot_w_scales.bitcast(I32)
        for q in range(QUADS):
            nc.sync.dma_start(slot_sc[quad_rows(q, 0, 4), :].bitcast(I32), slot_sc_hbm[0, 4 * q : 4 * q + 4, :])
        wgo_sb = held("wgo_sb", [P, S], F32)
        nc.sync.dma_start(wgo_sb[:], wgo)

        warm = keep.tile([P, 1], F32, name="warm")
        nc.vector.memset(warm[:], 0.0)
        warm_out = keep.tile([P, 1], F32, name="warm_out")
        nc.scalar.activation(warm_out[:], warm[:], ACT.Silu)

        for page in pages:
            nc.gpsimd.memset(page[:].bitcast(I32), 0)

        def round_weight(a, raw, copy):
            rounded = held("rounded%d" % a, [P, PACK, P, PACK], BF16, "scratch%d" % a)
            copy(rounded[:].rearrange("p t m j -> p m t j"), raw[:].rearrange("p j (m t) -> p m t j", t=PACK))
            return rounded

        def quantise_weight(name, rounded):
            codes = held(name + "_codes", [P, H], U32)
            scales = held(name + "_scales", [P, H], U8)
            nc.vector.quantize_mx(codes[:].bitcast(FP8X4), scales[:], rounded[:].rearrange("p t m j -> p (t m j)"))
            return codes, scales

        fam_bf = [round_weight(0, fam_raw[0], nc.scalar.copy)]

        fam_v = [held("fam_v%d" % a, [P, S], U32) for a in range(PASSES)]
        cand_v = [held("cand_v%d" % a, [P, S], U32) for a in range(PASSES)]
        for a in range(PASSES):
            nc.vector.tensor_copy(cand_v[a][:], tab_w[a][:].indirect(cand_list[:]))
            nc.vector.tensor_copy(fam_v[a][:], tab_w[a][:].indirect(fam_list[:]))
        fam_sc = held("fam_sc", [P, S], U8)
        cand_sc = [held("cand_sc%d" % a, [P, S], U8) for a in range(PASSES)]
        nc.vector.tensor_copy(fam_sc[:], tab_sc_both[:].indirect(fam_list[:]))
        nc.vector.tensor_copy(cand_sc[0][:], tab_sc_both[:].indirect(cand_list[:]))
        nc.vector.tensor_copy(cand_sc[1][:], tab_sc_last[:].indirect(cand_list[:]))

        fam_q = [quantise_weight("fam0", fam_bf[0])]
        fam_bf.append(round_weight(1, fam_raw[1], nc.vector.tensor_copy))
        fam_q.append(quantise_weight("fam1", fam_bf[1]))
        floor_bf = [round_weight(0, floor_raw[0], nc.vector.tensor_copy)]
        floor_q = [quantise_weight("floor0", floor_bf[0])]
        floor_bf.append(round_weight(1, floor_raw[1], nc.vector.tensor_copy))
        floor_q.append(quantise_weight("floor1", floor_bf[1]))

        identity = held("identity", [P, P], F32)
        make_identity(nc, identity[:])

        def family_product(acc, planes, ts, cols):
            for a in range(PASSES):
                codes, scales = planes[a]
                for i, t in enumerate(ts):
                    nc.tensor.matmul_mx(
                        acc[:, i, :],
                        lhsT=codes[:, t * P : (t + 1) * P].bitcast(FP8X4), lhsT_scale=scales[:, t * P : (t + 1) * P],
                        rhs=fam_v[a][:, cols].bitcast(FP8X4), rhs_scale=fam_sc[4 * a : P, cols],
                        start=(a == 0 and i == 0), stop=(a == PASSES - 1 and i == len(ts) - 1),
                    )

        def cand_tanh(c):
            cols = slice(c * CHUNK, (c + 1) * CHUNK)
            cand = psum.tile([CHUNK, H], F32, name="cand", tag="cand_then_low")
            for a in range(PASSES):
                nc.tensor.matmul_mx(
                    cand[:], lhsT=cand_v[a][:, cols].bitcast(FP8X4), lhsT_scale=cand_sc[a][:, cols],
                    rhs=cand_w[:, a, :].bitcast(FP4X4), rhs_scale=cand_w_sc[:, a, :],
                    start=(a == 0), stop=(a == PASSES - 1),
                )
            tanh_rows = held("tanh_rows%d" % c, [CHUNK, PACK, P], F32)
            nc.scalar.activation(tanh_rows[:], cand[:].rearrange("j (m t) -> j t m", t=PACK), ACT.Tanh)
            return tanh_rows

        h_codes = held("h_codes", [P, S], U32)
        h_scales = held("h_scales", [P, S], U8)

        def product_term(half, tanh_rows):
            cols = slice(half * HALF, (half + 1) * HALF)
            folded = held("folded", [P, PACK, HALF], F32)
            for t0 in (0, 2):
                fam = psum.tile([P, 2, HALF], F32, name="fam")
                family_product(fam, fam_q, (t0, t0 + 1), cols)
                nc.scalar.activation(folded[:, t0 : t0 + 2, :], fam[:], ACT.Abs, bias=-math.pi / 2)
            nc.scalar.activation(folded[:], folded[:], ACT.Abs, scale=-1.0, bias=math.pi)
            sin_f = ring.tile([P, PACK, HALF], F32, name="sin_f")
            nc.scalar.activation(sin_f[:], folded[:], ACT.Sin, bias=-math.pi / 2)
            prod = held("prod", [P, PACK, HALF], F32, "scratch1")
            for t0 in (0, 2):
                tanh_c = psum.tile([P, 2, HALF], F32, name="tanh_c")
                for i in range(2):
                    for c in range(2):
                        nc.tensor.transpose(
                            tanh_c[:, i, c * CHUNK : (c + 1) * CHUNK], tanh_rows[c][:, t0 + i, :], identity[:]
                        )
                for i in range(2):
                    t = t0 + i
                    nc.vector.scalar_tensor_tensor(
                        prod[:, t, :], sin_f[:, t, :], gain_sb[:, t : t + 1], tanh_c[:, i, :], ALU.mult, ALU.mult
                    )
            return prod

        def features(half, prod):
            h_bf = held("h_bf", [P, HALF, PACK], BF16, "scratch0")
            for c in range(2):
                first = half * HALF + c * CHUNK
                low = psum.tile([P, PACK, CHUNK], F32, name="low", tag="cand_then_low")
                family_product(low, floor_q, range(PACK), slice(first, first + CHUNK))
                inner = slice(c * CHUNK, (c + 1) * CHUNK)
                nc.vector.tensor_tensor(
                    h_bf[:, inner, :].rearrange("p (g i) t -> p g t i", i=4),
                    prod[:, :, inner].rearrange("p t (g i) -> p g t i", i=4),
                    low[:].rearrange("p t (g i) -> p g t i", i=4),
                    ALU.max,
                )
            cols = slice(half * HALF, (half + 1) * HALF)
            nc.vector.quantize_mx(
                h_codes[:, cols].bitcast(FP8X4), h_scales[:, cols], h_bf[:].rearrange("p n t -> p (n t)")
            )

        def place(n, first, widths):
            width = sum(widths)
            rows = slice(n * P, (n + 1) * P)
            acc = psum.tile([P, S], F32, name="e", tag="e")
            at = first
            for w in widths:
                nc.tensor.matmul_mx(
                    acc[:, at : at + w], lhsT=slot_w[:, rows].bitcast(FP8X4), lhsT_scale=slot_sc[:, rows],
                    rhs=h_codes[:, at : at + w].bitcast(FP8X4), rhs_scale=h_scales[:, at : at + w],
                    start=True, stop=True,
                )
                at = at + w
            cols = slice(first, first + width)
            th = ring.tile([P, S], F32, name="th")
            nc.scalar.activation(th[:, cols], acc[:, cols], ACT.Tanh, scale=0.5, bias=half_d[:, n : n + 1])
            y = ring.tile([P, S], F32, name="y")
            nc.scalar.activation(y[:, cols], th[:, cols], ACT.Copy, scale=0.5, bias=0.5)
            page = pages[n % PAGES]
            nc.vector.tensor_tensor(
                page[:].indirect(slot_list[:, first // 16 : (first + width) // 16]),
                y[:, cols], wgo_sb[:, cols], ALU.mult,
            )
            if first + width == S:
                nc.sync.dma_start(out[rows, :], page[:])

        half_d = keep.tile([P, ROW_TILES], F32, name="half_d")
        nc.vector.tensor_scalar(half_d[:], d_sb[:], 0.5, 0.0, ALU.mult, ALU.add)
        first = product_term(0, [cand_tanh(0), cand_tanh(1)])
        later_tanh = [cand_tanh(2), cand_tanh(3)]
        features(0, first)
        second = product_term(1, later_tanh)
        place(0, 0, [HALF])
        features(1, second)
        for n in range(1, PAGES):
            place(n, 0, [HALF])
        for n in range(PAGES):
            place(n, HALF, [HALF])
        for n in range(PAGES, ROW_TILES):
            place(n, 0, [S])
